import numpy as np
import ml_dtypes


def mxq(x, axis, fmt="e4m3"):
    dtype, down = {"e4m3": (ml_dtypes.float8_e4m3fn, 7), "e5m2": (ml_dtypes.float8_e5m2, 14)}[fmt]
    v = np.moveaxis(np.asarray(x, np.float32).astype(ml_dtypes.bfloat16).astype(np.float64), axis, -1)
    blocks = v.reshape(v.shape[:-1] + (-1, 32))
    amax = np.abs(blocks).max(-1, keepdims=True)
    byte = np.maximum(np.where(amax > 0, np.frexp(amax)[1] - 1 + 127, 0) - down, 1)
    scale = np.exp2(byte - 127.0)
    codes = (blocks / scale).astype(np.float32).astype(dtype).astype(np.float64)
    return np.moveaxis((codes * scale).reshape(v.shape), -1, axis)


WIDE = False


def mx_kscale(k):
    if not WIDE:
        return np.ones(k)
    levels = np.array([10, -10, 5, -5, 0])
    if k % 512:
        return np.exp2(np.random.permutation(np.resize(levels, k // 32))).repeat(32)
    a = np.empty((k // 512, 16))
    for p in range(k // 512):
        a[p, :8] = np.random.permutation(np.resize(levels, 8))
        for g in range(8):
            far = levels[np.abs(levels - a[p, g]) >= 10]
            a[p, g + 8] = far[np.random.randint(len(far))]
    return np.exp2(a.ravel()).repeat(32)


BF16 = ml_dtypes.bfloat16


def bf(x):
    return np.asarray(x, np.float32).astype(BF16)


def f64(x):
    return np.asarray(x).astype(np.float64)


N, D, K = 2048, 1024, 512


def scale_rows(gain, m):
    return gain[:, None] * m


def draw0():
    s = mx_kscale(D)
    u = mx_kscale(N)
    return {
        "x": bf(np.random.standard_normal((N, D)) * s),
        "p": bf(np.random.standard_normal((D, D)) / np.sqrt(D) / s[:, None]),
        "beta": bf(np.random.standard_normal((D, K)) / np.sqrt(D) / s[:, None]),
        "r": bf(np.random.uniform(0.5, 1.5, N) * u),
        "t": bf((1.0 + 0.3 * np.random.standard_normal(N)) / u),
        "v": bf(np.random.standard_normal((D, K)) / np.sqrt(D)),
        "psi": bf(np.random.uniform(0.05, 0.2, D)),
    }


def core(x, p, beta, r, t, v, psi):
    n_cases = x.shape[0]
    xq = mxq(f64(x), 1, "e4m3")
    e0 = xq @ mxq(f64(p), 0, "e4m3")
    e = scale_rows(f64(r), e0)
    z0 = xq @ mxq(f64(beta), 0, "e4m3")
    z = scale_rows(f64(t), z0)
    c = mxq(e, 0, "e4m3").T @ mxq(z, 0, "e4m3")
    return (c / n_cases - f64(v)) / f64(psi)[:, None]


def e4m3fn_bytes(y):
    return np.clip(np.asarray(y, np.float64), -448.0, 448.0).astype(np.float32).astype(ml_dtypes.float8_e4m3fn).view(np.uint8)


def e4m3fn_values(b):
    return np.asarray(b, np.uint8).view(ml_dtypes.float8_e4m3fn).astype(np.float64)


def setup_inputs():
    d = draw0()
    x0 = np.asarray(d['x']).astype(np.float64)
    s = (np.max(np.abs(x0), axis=(0,), keepdims=True) / 448.0).astype(np.float32)
    out = {}
    for k, v in d.items():
        if k == 'x':
            out['x_bytes'] = e4m3fn_bytes(x0 / s.astype(np.float64))
            out['x_scale'] = s
        else:
            out[k] = v
    return out


def reference(x_bytes, x_scale, p, beta, r, t, v, psi):
    return core(e4m3fn_values(x_bytes) * x_scale.astype(np.float64), p, beta, r, t, v, psi)

@@ -1,0 +1,312 @@
+from contextlib import ExitStack
+
+import concourse.mybir as mybir
+from concourse.masks import make_identity
+
+N, D, K = 2048, 1024, 512
+
+FLOPS = 2 * N * D * D + 2 * N * D * K + 2 * N * D * K
+
+F32 = mybir.dt.float32
+BF16 = mybir.dt.bfloat16
+U32 = mybir.dt.uint32
+U8 = mybir.dt.uint8
+FP8 = mybir.dt.float8_e4m3fn
+FP8X4 = mybir.dt.float8_e4m3fn_x4
+MULT = mybir.AluOpType.mult
+SUBTRACT = mybir.AluOpType.subtract
+COPY = mybir.ActivationFunctionType.Copy
+
+P = 128
+PACK = 4
+K_PASS = P * PACK
+PASSES = D // K_PASS
+GROUPS = N // K_PASS
+UNITS = N // P
+WIDTH = 512
+BLOCKS = (D + K) // WIDTH
+Z = BLOCKS - 1
+D_BLOCKS = D // P
+WIDE_BUFS = 12
+FLAT_BUFS = 2
+FIRST_SCALED_V = 4
+KINDS = ["factors","accumulate","multiply","x_quantize","wz_group","turn","finish","empty","prepare_v","y_quantize","w_quantize","y_group","w_group","x_group","product","psi"]
+W_AT = {(0, 0): -59, (0, 1): -56, (Z, 0): -37, (Z, 1): -26, (1, 0): -6, (1, 1): 4}
+WQ_AT = {(0, 0): -36, (0, 1): -11, (Z, 0): 1, (Z, 1): 1, (1, 0): 3, (1, 1): 5}
+P_AT, P_STEP, T_AT, T_STEP, Q_LAG = -14, 1.5, -11, 1.5, 7
+I_LAG, Y_LAG, C_LAG, F_AT, V_AT, V_STEP, PSI_AT = 10, 8, 43, 199, 4, 15, -8
+
+
+def tile_factoranalysisemloadinggradient_kernel(
+    tc, x_bytes, x_scale, p, beta, r, t, v, psi, out
+):
+    nc = tc.nc
+    with ExitStack() as ctx:
+        keep = ctx.enter_context(tc.tile_pool(name="keep", bufs=1))
+        work = ctx.enter_context(tc.tile_pool(name="work", bufs=3))
+        sums = ctx.enter_context(tc.psum_pool(name="sums", bufs=1))
+        banks = ctx.enter_context(tc.psum_pool(name="banks", bufs=4))
+        ctx.enter_context(tc.manual_schedule())
+
+        warm = keep.tile([P, 1], F32, name="warm")
+        nc.vector.memset(warm[:], 0.0)
+        nc.scalar.activation(out=warm[:], in_=warm[:], func=COPY)
+        identity = keep.tile([P, P], F32, name="identity")
+        make_identity(nc, identity[:])
+        identity16 = keep.tile([P, P], BF16, name="identity16")
+        nc.gpsimd.tensor_copy(out=identity16[:], in_=identity[:])
+        psi_rows = keep.tile([P, P], BF16, name="psi_rows")
+        nc.gpsimd.memset(psi_rows[:], 0.0)
+
+        scale_cols = keep.tile([P, D // P], F32, name="scale_cols")
+        nc.sync.dma_start(out=scale_cols[:], in_=x_scale.rearrange("o (p m) -> p (o m)", p=P))
+        r16 = keep.tile([P, GROUPS, PACK], BF16, name="r16")
+        nc.scalar.dma_start(out=r16[:], in_=r.rearrange("(g p t) -> p g t", p=P, t=PACK))
+        t16 = keep.tile([P, GROUPS, PACK], BF16, name="t16")
+        nc.scalar.dma_start(out=t16[:], in_=t.rearrange("(g p t) -> p g t", p=P, t=PACK))
+
+        x_view = x_bytes.rearrange("(g p t) f -> g p t f", p=P, t=PACK)
+        p_view = p.rearrange("(g p j) d -> g p j d", p=P, j=PACK)
+        beta_view = beta.rearrange("(g p j) d -> g p j d", p=P, j=PACK)
+        x_raw = []
+        for g in range(GROUPS):
+            raw = keep.tile([P, PACK, D], U8, name=f"x_raw{g}")
+            x_raw.append(raw)
+        w_raw = {}
+        for b in range(BLOCKS):
+            for g in range(PASSES):
+                raw = keep.tile([P, PACK, WIDTH], BF16, name=f"w_raw{b}{g}")
+                w_raw[b, g] = raw
+
+        def load_x(g, a, b):
+            nc.sync.dma_start(out=x_raw[g][:, a:b, :], in_=x_view[g][:, a:b, :])
+
+        def load_w(b, g):
+            if b == Z:
+                src = beta_view[g]
+            else:
+                src = p_view[g][:, :, b * WIDTH : (b + 1) * WIDTH]
+            nc.sync.dma_start(out=w_raw[b, g][:], in_=src)
+
+        load_w(0, 0)
+        load_x(0, 0, 2)
+        load_w(0, 1)
+        load_x(0, 2, 4)
+        nc.sync.dma_start(out=psi_rows[0:D_BLOCKS, :], in_=psi.rearrange("(b p) -> b p", p=P))
+        load_w(Z, 0)
+        load_w(Z, 1)
+        load_x(1, 0, 4)
+        load_w(1, 0)
+        load_w(1, 1)
+        load_x(2, 0, 4)
+        load_x(3, 0, 4)
+        v_raw = keep.tile([P, D_BLOCKS, K], BF16, name="v_raw")
+        nc.sync.dma_start(out=v_raw[:], in_=v.rearrange("(b p) k -> p b k", p=P))
+
+        scale = keep.tile([P, D], F32, name="scale")
+        w_codes = keep.tile([P, BLOCKS, PASSES, WIDTH], U32, name="w_codes", align_bytes=256)
+        w_planes = keep.tile([P, BLOCKS, PASSES, WIDTH], U8, name="w_planes", align_bytes=256)
+        x_codes = keep.tile([P, UNITS, PASSES, P], U32, name="x_codes", align_bytes=256)
+        x_planes = keep.tile([P, UNITS, PASSES, P], U8, name="x_planes", align_bytes=256)
+        y_codes = keep.tile([P, GROUPS, BLOCKS, WIDTH], U32, name="y_codes", align_bytes=256)
+        y_planes = keep.tile([P, GROUPS, BLOCKS, WIDTH], U8, name="y_planes", align_bytes=256)
+        factor_r = keep.tile([P, UNITS], F32, name="factor_r")
+        factor_t = keep.tile([P, UNITS], F32, name="factor_t")
+        v_scaled = keep.tile([P, D_BLOCKS - FIRST_SCALED_V, K], F32, name="v_scaled")
+        psi_inv_mean = keep.tile([P, D_BLOCKS], F32, name="psi_inv_mean")
+        psi_inv = keep.tile([P, D_BLOCKS], F32, name="psi_inv")
+
+        w_grouped, wide, turned, x_grouped = {}, {}, {}, {}
+        y_bank, y_flat, y_grouped, c_bank = {}, {}, {}, {}
+
+        def spread_scale():
+            view = scale[:].rearrange("p (n q m) -> p q n m", q=2, m=4)
+            for q, copy in ((0, nc.vector.tensor_copy), (1, nc.scalar.copy)):
+                bank = banks.tile([P, 4, P], F32, name="bank")
+                for m in range(4):
+                    col = scale_cols[:, 4 * q + m : 4 * q + m + 1]
+                    nc.tensor.transpose(bank[:, m, :], col.to_broadcast([P, P]), identity[:])
+                copy(out=view[:, q], in_=bank[:].rearrange("p m n -> p n m"))
+
+        def w_group(b, g, copy):
+            tile = work.tile([P, WIDTH, PACK], BF16, name="w_grouped_tile", align_bytes=256)
+            copy(out=tile[:], in_=w_raw[b, g][:].rearrange("p j c -> p c j"))
+            w_grouped[b, g] = tile
+
+        def w_quantize(b, g):
+            nc.vector.quantize_mx(
+                out=w_codes[:, b, g, :].bitcast(FP8X4),
+                scales=w_planes[:, b, g, :],
+                in_=w_grouped[b, g][:].rearrange("p c j -> p (c j)"),
+            )
+
+        def product(i):
+            tile = work.tile([P, D], BF16, name="wide_tile", bufs=WIDE_BUFS)
+            nc.vector.tensor_tensor(
+                out=tile[:],
+                in0=x_raw[i // PACK][:, i % PACK, :].bitcast(FP8),
+                in1=scale[:],
+                op=MULT,
+            )
+            wide[i] = tile
+
+        def turn(i):
+            bank = banks.tile([P, PASSES, 2, P], F32, name="bank")
+            words = wide[i][:].bitcast(F32)
+            for g in range(PASSES):
+                for u in range(2):
+                    nc.tensor.transpose(
+                        bank[:, g, u, :], words[:, 256 * g + u : 256 * (g + 1) : 2], identity[:]
+                    )
+            turned[i] = bank
+
+        def x_group(i):
+            tile = work.tile([P, PASSES * P * PACK], BF16, name="x_grouped_tile", bufs=6, align_bytes=256)
+            nc.scalar.copy(
+                out=tile[:].bitcast(F32).rearrange("p (g c u) -> p g c u", g=PASSES, u=2),
+                in_=turned[i][:].rearrange("p g u c -> p g c u"),
+            )
+            x_grouped[i] = tile
+
+        def x_quantize(i):
+            nc.vector.quantize_mx(
+                out=x_codes[:, i].rearrange("p g c -> p (g c)").bitcast(FP8X4),
+                scales=x_planes[:, i].rearrange("p g c -> p (g c)"),
+                in_=x_grouped[i][:],
+            )
+
+        def multiply(i, b):
+            bank = banks.tile([P, WIDTH], F32, name="bank")
+            for g in range(PASSES):
+                nc.tensor.matmul_mx(
+                    out=bank[:],
+                    lhsT=x_codes[:, i, g, :].bitcast(FP8X4),
+                    lhsT_scale=x_planes[:, i, g, :],
+                    rhs=w_codes[:, b, g, :].bitcast(FP8X4),
+                    rhs_scale=w_planes[:, b, g, :],
+                    start=(g == 0),
+                    stop=(g == PASSES - 1),
+                )
+            y_bank[i, b] = bank
+
+        def empty(i, b):
+            group, j = i // PACK, i % PACK
+            if j == 0:
+                tile = work.tile([P, PACK, WIDTH], BF16, name=f"y_flat_tile{b}", bufs=FLAT_BUFS)
+                y_flat[group, b] = tile
+            factor = factor_t if b == Z else factor_r
+            nc.scalar.activation(
+                out=y_flat[group, b][:, j, :], in_=y_bank[i, b][:], func=COPY, scale=factor[:, i : i + 1]
+            )
+
+        def y_group(group, b):
+            tile = work.tile([P, WIDTH, PACK], BF16, name="y_grouped_tile", align_bytes=256)
+            nc.vector.tensor_copy(out=tile[:], in_=y_flat[group, b][:].rearrange("p j c -> p c j"))
+            y_grouped[group, b] = tile
+
+        def y_quantize(group, b):
+            nc.vector.quantize_mx(
+                out=y_codes[:, group, b, :].bitcast(FP8X4),
+                scales=y_planes[:, group, b, :],
+                in_=y_grouped[group, b][:].rearrange("p c j -> p (c j)"),
+            )
+
+        def accumulate(group, d):
+            if group == 0:
+                if d < 4:
+                    bank = sums.tile([P, K], F32, name=f"c{d}")
+                else:
+                    bank = banks.tile([P, K], F32, name="bank")
+                c_bank[d] = bank
+            cols = slice(d % 4 * P, (d % 4 + 1) * P)
+            nc.tensor.matmul_mx(
+                out=c_bank[d][:],
+                lhsT=y_codes[:, group, d // 4, cols].bitcast(FP8X4),
+                lhsT_scale=y_planes[:, group, d // 4, cols],
+                rhs=y_codes[:, group, Z, :].bitcast(FP8X4),
+                rhs_scale=y_planes[:, group, Z, :],
+                start=(group == 0),
+                stop=(group == GROUPS - 1),
+            )
+
+        def prepare_psi():
+            bank = banks.tile([P, P], BF16, name="bank")
+            nc.tensor.transpose(bank[:], psi_rows[:], identity16[:])
+            nc.vector.reciprocal(out=psi_inv[:], in_=bank[:, 0:D_BLOCKS])
+            nc.vector.tensor_scalar(
+                out=psi_inv_mean[:], in0=psi_inv[:], scalar1=1.0 / N, scalar2=None, op0=MULT
+            )
+
+        def prepare_v(d):
+            nc.scalar.activation(
+                out=v_scaled[:, d - FIRST_SCALED_V, :], in_=v_raw[:, d, :], func=COPY, scale=psi_inv[:, d : d + 1]
+            )
+
+        def finish(d):
+            tile = work.tile([P, K], F32, name="result", bufs=4)
+            if d < FIRST_SCALED_V:
+                nc.vector.scalar_tensor_tensor(
+                    out=tile[:], in0=c_bank[d][:], scalar=1.0 / N, in1=v_raw[:, d, :], op0=MULT, op1=SUBTRACT
+                )
+                nc.scalar.activation(out=tile[:], in_=tile[:], func=COPY, scale=psi_inv[:, d : d + 1])
+            else:
+                nc.vector.scalar_tensor_tensor(
+                    out=tile[:],
+                    in0=c_bank[d][:],
+                    scalar=psi_inv_mean[:, d : d + 1],
+                    in1=v_scaled[:, d - FIRST_SCALED_V, :],
+                    op0=MULT,
+                    op1=SUBTRACT,
+                )
+            nc.sync.dma_start(out=out[d * P : (d + 1) * P, :], in_=tile[:])
+
+        vector_copy = nc.vector.tensor_copy
+        scalar_copy = nc.scalar.copy
+
+        def factors():
+            nc.vector.tensor_copy(out=factor_r[:], in_=r16[:].rearrange("p g t -> p (g t)"))
+            nc.vector.tensor_copy(out=factor_t[:], in_=t16[:].rearrange("p g t -> p (g t)"))
+
+        calls = []
+
+        def at(tick, kind, f, *args):
+            calls.append((tick, KINDS.index(kind), len(calls), f, args))
+
+        order = (0, Z, 1)
+        place = {}
+        for g in range(GROUPS):
+            for b in order:
+                for j in range(PACK):
+                    place[g * PACK + j, b] = len(place)
+        for (b, g, copy) in ((0, 0, vector_copy), (0, 1, vector_copy), (Z, 0, scalar_copy), (Z, 1, scalar_copy), (1, 0, scalar_copy), (1, 1, scalar_copy)):
+            at(W_AT[b, g], "w_group" if b != Z else "wz_group", w_group, b, g, copy)
+            at(WQ_AT[b, g], "w_quantize", w_quantize, b, g)
+        for i in range(UNITS):
+            at(P_AT + P_STEP * i, "product", product, i)
+            at(T_AT + T_STEP * i, "turn", turn, i)
+            at(T_AT + T_STEP * i, "x_group", x_group, i)
+            at(T_AT + T_STEP * i + Q_LAG, "x_quantize", x_quantize, i)
+        for (i, b), n in place.items():
+            at(n, "multiply", multiply, i, b)
+            at(n, "empty", empty, i, b)
+        for g in range(GROUPS):
+            for b in order:
+                n = place[g * PACK + PACK - 1, b] + I_LAG
+                at(n, "y_group", y_group, g, b)
+                at(n + Y_LAG, "y_quantize", y_quantize, g, b)
+            n = place[g * PACK + PACK - 1, Z] + I_LAG + Y_LAG + C_LAG
+            for d in range(4):
+                at(n + 0.25 * d, "accumulate", accumulate, g, d)
+        for d in range(4):
+            at(F_AT + d, "finish", finish, d)
+        for d in range(4, 8):
+            for g in range(GROUPS - 1):
+                at(200 + d + 0.1 * g, "accumulate", accumulate, g, d)
+            at(210 + d, "accumulate", accumulate, GROUPS - 1, d)
+            at(210 + d, "finish", finish, d)
+            at(V_AT + V_STEP * d, "prepare_v", prepare_v, d)
+        at(PSI_AT, "psi", prepare_psi)
+        at(-99, "factors", factors)
+        spread_scale()
+        for tick, kind, n, f, args in sorted(calls, key=lambda c: c[:3]):
+            f(*args)

@@ -24,17 +24,19 @@ PASSES = D // K_PASS
 GROUPS = N // K_PASS
 UNITS = N // P
 WIDTH = 512
+HALF = WIDTH // 2
 BLOCKS = (D + K) // WIDTH
 Z = BLOCKS - 1
 D_BLOCKS = D // P
+
 WIDE_BUFS = 12
-FLAT_BUFS = 2
-FIRST_SCALED_V = 4
-KINDS = ["factors","accumulate","multiply","x_quantize","wz_group","turn","finish","empty","prepare_v","y_quantize","w_quantize","y_group","w_group","x_group","product","psi"]
-W_AT = {(0, 0): -59, (0, 1): -56, (Z, 0): -37, (Z, 1): -26, (1, 0): -6, (1, 1): 4}
-WQ_AT = {(0, 0): -36, (0, 1): -11, (Z, 0): 1, (Z, 1): 1, (1, 0): 3, (1, 1): 5}
-P_AT, P_STEP, T_AT, T_STEP, Q_LAG = -14, 1.5, -11, 1.5, 7
-I_LAG, Y_LAG, C_LAG, F_AT, V_AT, V_STEP, PSI_AT = 10, 8, 43, 199, 4, 15, -8
+FIRST_SCALED_V = 6
+ORDER = (0, Z, 1)
+KINDS = ["w_group","psi","product","w_quantize","multiply","empty","y_quantize","x_quantize","turn","wz_group","y_group","x_group"]
+W_AT = {(0, 0): -42, (0, 1): -70, (2, 0): -28, (2, 1): -16, (1, 0): 6, (1, 1): -14}
+WQ_AT = {(0, 0): -9, (0, 1): -10, (2, 0): 1, (2, 1): -5, (1, 0): 11, (1, 1): 5}
+P_AT, P_STEP, T_AT, T_STEP, Q_LAG, I_LAG, Y_LAG, PSI_AT = -29, 2.75, -22, 3.0, 8, 8, 4, 32
+SHIFT = {0: 0, Z: 3, 1: 15}
 
 
 def tile_factoranalysisemloadinggradient_kernel(
@@ -44,8 +46,7 @@ def tile_factoranalysisemloadinggradient_kernel(
     with ExitStack() as ctx:
         keep = ctx.enter_context(tc.tile_pool(name="keep", bufs=1))
         work = ctx.enter_context(tc.tile_pool(name="work", bufs=3))
-        sums = ctx.enter_context(tc.psum_pool(name="sums", bufs=1))
-        banks = ctx.enter_context(tc.psum_pool(name="banks", bufs=4))
+        banks = ctx.enter_context(tc.psum_pool(name="banks", bufs=8))
         ctx.enter_context(tc.manual_schedule())
 
         warm = keep.tile([P, 1], F32, name="warm")
@@ -75,24 +76,30 @@ def tile_factoranalysisemloadinggradient_kernel(
         w_raw = {}
         for b in range(BLOCKS):
             for g in range(PASSES):
-                raw = keep.tile([P, PACK, WIDTH], BF16, name=f"w_raw{b}{g}")
-                w_raw[b, g] = raw
+                if (b, g) != (0, 0):
+                    raw = keep.tile([P, PACK, WIDTH], BF16, name=f"w_raw{b}{g}")
+                    w_raw[b, g] = raw
+        first_halves = []
+        for half in range(2):
+            raw = keep.tile([P, PACK, HALF], BF16, name=f"first_half{half}")
+            first_halves.append(raw)
 
         def load_x(g, a, b):
             nc.sync.dma_start(out=x_raw[g][:, a:b, :], in_=x_view[g][:, a:b, :])
 
         def load_w(b, g):
-            if b == Z:
-                src = beta_view[g]
-            else:
-                src = p_view[g][:, :, b * WIDTH : (b + 1) * WIDTH]
+            src = beta_view[g] if b == Z else p_view[g][:, :, b * WIDTH : (b + 1) * WIDTH]
             nc.sync.dma_start(out=w_raw[b, g][:], in_=src)
 
-        load_w(0, 0)
+        def load_first(half):
+            cols = slice(half * HALF, (half + 1) * HALF)
+            nc.sync.dma_start(out=first_halves[half][:], in_=p_view[0][:, :, cols])
+
+        load_first(0)
         load_x(0, 0, 2)
+        load_first(1)
         load_w(0, 1)
         load_x(0, 2, 4)
-        nc.sync.dma_start(out=psi_rows[0:D_BLOCKS, :], in_=psi.rearrange("(b p) -> b p", p=P))
         load_w(Z, 0)
         load_w(Z, 1)
         load_x(1, 0, 4)
@@ -100,6 +107,7 @@ def tile_factoranalysisemloadinggradient_kernel(
         load_w(1, 1)
         load_x(2, 0, 4)
         load_x(3, 0, 4)
+        nc.sync.dma_start(out=psi_rows[0:D_BLOCKS, :], in_=psi.rearrange("(b p) -> b p", p=P))
         v_raw = keep.tile([P, D_BLOCKS, K], BF16, name="v_raw")
         nc.sync.dma_start(out=v_raw[:], in_=v.rearrange("(b p) k -> p b k", p=P))
 
@@ -112,25 +120,40 @@ def tile_factoranalysisemloadinggradient_kernel(
         y_planes = keep.tile([P, GROUPS, BLOCKS, WIDTH], U8, name="y_planes", align_bytes=256)
         factor_r = keep.tile([P, UNITS], F32, name="factor_r")
         factor_t = keep.tile([P, UNITS], F32, name="factor_t")
-        v_scaled = keep.tile([P, D_BLOCKS - FIRST_SCALED_V, K], F32, name="v_scaled")
-        psi_inv_mean = keep.tile([P, D_BLOCKS], F32, name="psi_inv_mean")
         psi_inv = keep.tile([P, D_BLOCKS], F32, name="psi_inv")
+        psi_inv_mean = keep.tile([P, D_BLOCKS], F32, name="psi_inv_mean")
+        v_scaled = keep.tile([P, D_BLOCKS - FIRST_SCALED_V, K], F32, name="v_scaled")
 
         w_grouped, wide, turned, x_grouped = {}, {}, {}, {}
-        y_bank, y_flat, y_grouped, c_bank = {}, {}, {}, {}
+        y_bank, y_flat, y_grouped = {}, {}, {}
+        vector_copy = nc.vector.tensor_copy
+        scalar_copy = nc.scalar.copy
 
         def spread_scale():
             view = scale[:].rearrange("p (n q m) -> p q n m", q=2, m=4)
-            for q, copy in ((0, nc.vector.tensor_copy), (1, nc.scalar.copy)):
+            for q, copy in ((0, vector_copy), (1, scalar_copy)):
                 bank = banks.tile([P, 4, P], F32, name="bank")
                 for m in range(4):
                     col = scale_cols[:, 4 * q + m : 4 * q + m + 1]
                     nc.tensor.transpose(bank[:, m, :], col.to_broadcast([P, P]), identity[:])
                 copy(out=view[:, q], in_=bank[:].rearrange("p m n -> p n m"))
 
+        def interleave(copy, dst, src):
+            copy(
+                out=dst.rearrange("p (c i) j -> p c j i", i=4),
+                in_=src.rearrange("p j (c i) -> p c j i", i=4),
+            )
+
+        def w_group_first(half):
+            if half == 0:
+                tile = work.tile([P, WIDTH, PACK], BF16, name="w_grouped_tile", bufs=5, align_bytes=256)
+                w_grouped[0, 0] = tile
+            dst = w_grouped[0, 0][:, half * HALF : (half + 1) * HALF, :]
+            interleave(vector_copy, dst, first_halves[half][:])
+
         def w_group(b, g, copy):
-            tile = work.tile([P, WIDTH, PACK], BF16, name="w_grouped_tile", align_bytes=256)
-            copy(out=tile[:], in_=w_raw[b, g][:].rearrange("p j c -> p c j"))
+            tile = work.tile([P, WIDTH, PACK], BF16, name="w_grouped_tile", bufs=5, align_bytes=256)
+            interleave(copy, tile[:], w_raw[b, g][:])
             w_grouped[b, g] = tile
 
         def w_quantize(b, g):
@@ -161,18 +184,19 @@ def tile_factoranalysisemloadinggradient_kernel(
             turned[i] = bank
 
         def x_group(i):
-            tile = work.tile([P, PASSES * P * PACK], BF16, name="x_grouped_tile", bufs=6, align_bytes=256)
+            if i % 2 == 0:
+                tile = work.tile([P, 2, PASSES * P * PACK], BF16, name="x_grouped_tile", align_bytes=256)
+                x_grouped[i // 2] = tile
             nc.scalar.copy(
-                out=tile[:].bitcast(F32).rearrange("p (g c u) -> p g c u", g=PASSES, u=2),
+                out=x_grouped[i // 2][:, i % 2, :].bitcast(F32).rearrange("p (g c u) -> p g c u", g=PASSES, u=2),
                 in_=turned[i][:].rearrange("p g u c -> p g c u"),
             )
-            x_grouped[i] = tile
 
-        def x_quantize(i):
+        def x_quantize(k):
             nc.vector.quantize_mx(
-                out=x_codes[:, i].rearrange("p g c -> p (g c)").bitcast(FP8X4),
-                scales=x_planes[:, i].rearrange("p g c -> p (g c)"),
-                in_=x_grouped[i][:],
+                out=x_codes[:, 2 * k : 2 * k + 2].rearrange("p u g c -> p (u g c)").bitcast(FP8X4),
+                scales=x_planes[:, 2 * k : 2 * k + 2].rearrange("p u g c -> p (u g c)"),
+                in_=x_grouped[k][:].rearrange("p u n -> p (u n)"),
             )
 
         def multiply(i, b):
@@ -192,7 +216,7 @@ def tile_factoranalysisemloadinggradient_kernel(
         def empty(i, b):
             group, j = i // PACK, i % PACK
             if j == 0:
-                tile = work.tile([P, PACK, WIDTH], BF16, name=f"y_flat_tile{b}", bufs=FLAT_BUFS)
+                tile = work.tile([P, PACK, WIDTH], BF16, name=f"y_flat_tile{b}", bufs=2)
                 y_flat[group, b] = tile
             factor = factor_t if b == Z else factor_r
             nc.scalar.activation(
@@ -201,7 +225,7 @@ def tile_factoranalysisemloadinggradient_kernel(
 
         def y_group(group, b):
             tile = work.tile([P, WIDTH, PACK], BF16, name="y_grouped_tile", align_bytes=256)
-            nc.vector.tensor_copy(out=tile[:], in_=y_flat[group, b][:].rearrange("p j c -> p c j"))
+            interleave(vector_copy, tile[:], y_flat[group, b][:])
             y_grouped[group, b] = tile
 
         def y_quantize(group, b):
@@ -211,16 +235,10 @@ def tile_factoranalysisemloadinggradient_kernel(
                 in_=y_grouped[group, b][:].rearrange("p c j -> p (c j)"),
             )
 
-        def accumulate(group, d):
-            if group == 0:
-                if d < 4:
-                    bank = sums.tile([P, K], F32, name=f"c{d}")
-                else:
-                    bank = banks.tile([P, K], F32, name="bank")
-                c_bank[d] = bank
+        def accumulate(bank, group, d):
             cols = slice(d % 4 * P, (d % 4 + 1) * P)
             nc.tensor.matmul_mx(
-                out=c_bank[d][:],
+                out=bank[:],
                 lhsT=y_codes[:, group, d // 4, cols].bitcast(FP8X4),
                 lhsT_scale=y_planes[:, group, d // 4, cols],
                 rhs=y_codes[:, group, Z, :].bitcast(FP8X4),
@@ -242,17 +260,17 @@ def tile_factoranalysisemloadinggradient_kernel(
                 out=v_scaled[:, d - FIRST_SCALED_V, :], in_=v_raw[:, d, :], func=COPY, scale=psi_inv[:, d : d + 1]
             )
 
-        def finish(d):
-            tile = work.tile([P, K], F32, name="result", bufs=4)
+        def finish(bank, d):
+            tile = work.tile([P, K], F32, name="result", tag="wide_tile", bufs=WIDE_BUFS)
             if d < FIRST_SCALED_V:
                 nc.vector.scalar_tensor_tensor(
-                    out=tile[:], in0=c_bank[d][:], scalar=1.0 / N, in1=v_raw[:, d, :], op0=MULT, op1=SUBTRACT
+                    out=tile[:], in0=bank[:], scalar=1.0 / N, in1=v_raw[:, d, :], op0=MULT, op1=SUBTRACT
                 )
                 nc.scalar.activation(out=tile[:], in_=tile[:], func=COPY, scale=psi_inv[:, d : d + 1])
             else:
                 nc.vector.scalar_tensor_tensor(
                     out=tile[:],
-                    in0=c_bank[d][:],
+                    in0=bank[:],
                     scalar=psi_inv_mean[:, d : d + 1],
                     in1=v_scaled[:, d - FIRST_SCALED_V, :],
                     op0=MULT,
@@ -260,53 +278,60 @@ def tile_factoranalysisemloadinggradient_kernel(
                 )
             nc.sync.dma_start(out=out[d * P : (d + 1) * P, :], in_=tile[:])
 
-        vector_copy = nc.vector.tensor_copy
-        scalar_copy = nc.scalar.copy
-
-        def factors():
-            nc.vector.tensor_copy(out=factor_r[:], in_=r16[:].rearrange("p g t -> p (g t)"))
-            nc.vector.tensor_copy(out=factor_t[:], in_=t16[:].rearrange("p g t -> p (g t)"))
-
         calls = []
 
         def at(tick, kind, f, *args):
             calls.append((tick, KINDS.index(kind), len(calls), f, args))
 
-        order = (0, Z, 1)
         place = {}
         for g in range(GROUPS):
-            for b in order:
+            for b in ORDER:
                 for j in range(PACK):
-                    place[g * PACK + j, b] = len(place)
-        for (b, g, copy) in ((0, 0, vector_copy), (0, 1, vector_copy), (Z, 0, scalar_copy), (Z, 1, scalar_copy), (1, 0, scalar_copy), (1, 1, scalar_copy)):
-            at(W_AT[b, g], "w_group" if b != Z else "wz_group", w_group, b, g, copy)
+                    shift = SHIFT[b] if g < GROUPS - 1 else 0
+                    place[g * PACK + j, b] = len(place) + shift
+        for b, g in W_AT:
+            if (b, g) == (0, 0):
+                at(W_AT[b, g], "w_group", w_group_first, 1)
+            else:
+                copy = scalar_copy
+                at(W_AT[b, g], "w_group" if b != Z else "wz_group", w_group, b, g, copy)
             at(WQ_AT[b, g], "w_quantize", w_quantize, b, g)
         for i in range(UNITS):
             at(P_AT + P_STEP * i, "product", product, i)
-            at(T_AT + T_STEP * i, "turn", turn, i)
-            at(T_AT + T_STEP * i, "x_group", x_group, i)
-            at(T_AT + T_STEP * i + Q_LAG, "x_quantize", x_quantize, i)
+            if i % 2 == 0:
+                at(T_AT + T_STEP * (i + 1) + Q_LAG, "x_quantize", x_quantize, i // 2)
+            at(T_AT + T_STEP * (i - i % 2), "turn", turn, i)
+            at(T_AT + T_STEP * (i - i % 2), "x_group", x_group, i)
         for (i, b), n in place.items():
             at(n, "multiply", multiply, i, b)
             at(n, "empty", empty, i, b)
         for g in range(GROUPS):
-            for b in order:
+            for b in ORDER:
                 n = place[g * PACK + PACK - 1, b] + I_LAG
                 at(n, "y_group", y_group, g, b)
                 at(n + Y_LAG, "y_quantize", y_quantize, g, b)
-            n = place[g * PACK + PACK - 1, Z] + I_LAG + Y_LAG + C_LAG
-            for d in range(4):
-                at(n + 0.25 * d, "accumulate", accumulate, g, d)
-        for d in range(4):
-            at(F_AT + d, "finish", finish, d)
-        for d in range(4, 8):
-            for g in range(GROUPS - 1):
-                at(200 + d + 0.1 * g, "accumulate", accumulate, g, d)
-            at(210 + d, "accumulate", accumulate, GROUPS - 1, d)
-            at(210 + d, "finish", finish, d)
-            at(V_AT + V_STEP * d, "prepare_v", prepare_v, d)
         at(PSI_AT, "psi", prepare_psi)
-        at(-99, "factors", factors)
+
+        w_group_first(0)
         spread_scale()
+        vector_copy(out=factor_r[:], in_=r16[:].rearrange("p g t -> p (g t)"))
+        vector_copy(out=factor_t[:], in_=t16[:].rearrange("p g t -> p (g t)"))
         for tick, kind, n, f, args in sorted(calls, key=lambda c: c[:3]):
             f(*args)
+
+        for d in range(FIRST_SCALED_V, D_BLOCKS):
+            prepare_v(d)
+        first = []
+        for d in range(4):
+            bank = banks.tile([P, K], F32, name="bank")
+            first.append(bank)
+        for g in range(GROUPS):
+            for d in range(4):
+                accumulate(first[d], g, d)
+        for d in range(4):
+            finish(first[d], d)
+        for d in range(4, D_BLOCKS):
+            bank = banks.tile([P, K], F32, name="bank")
+            for g in range(GROUPS):
+                accumulate(bank, g, d)
+            finish(bank, d)

from contextlib import ExitStack

import concourse.mybir as mybir
from concourse.masks import make_identity

N, D, K = 2048, 1024, 512

FLOPS = 2 * N * D * D + 2 * N * D * K + 2 * N * D * K

F32 = mybir.dt.float32
BF16 = mybir.dt.bfloat16
U32 = mybir.dt.uint32
U8 = mybir.dt.uint8
FP8 = mybir.dt.float8_e4m3fn
FP8X4 = mybir.dt.float8_e4m3fn_x4
MULT = mybir.AluOpType.mult
SUBTRACT = mybir.AluOpType.subtract
COPY = mybir.ActivationFunctionType.Copy

P = 128
PACK = 4
K_PASS = P * PACK
PASSES = D // K_PASS
GROUPS = N // K_PASS
UNITS = N // P
WIDTH = 512
HALF = WIDTH // 2
BLOCKS = (D + K) // WIDTH
Z = BLOCKS - 1
D_BLOCKS = D // P

WIDE_BUFS = 12
FIRST_SCALED_V = 6
ORDER = (0, Z, 1)
KINDS = ["w_group","psi","product","w_quantize","multiply","empty","y_quantize","x_quantize","turn","wz_group","y_group","x_group"]
W_AT = {(0, 0): -42, (0, 1): -70, (2, 0): -28, (2, 1): -16, (1, 0): 6, (1, 1): -14}
WQ_AT = {(0, 0): -9, (0, 1): -10, (2, 0): 1, (2, 1): -5, (1, 0): 11, (1, 1): 5}
P_AT, P_STEP, T_AT, T_STEP, Q_LAG, I_LAG, Y_LAG, PSI_AT = -29, 2.75, -22, 3.0, 8, 8, 4, 32
SHIFT = {0: 0, Z: 3, 1: 15}


def tile_factoranalysisemloadinggradient_kernel(
    tc, x_bytes, x_scale, p, beta, r, t, v, psi, out
):
    nc = tc.nc
    with ExitStack() as ctx:
        keep = ctx.enter_context(tc.tile_pool(name="keep", bufs=1))
        work = ctx.enter_context(tc.tile_pool(name="work", bufs=3))
        banks = ctx.enter_context(tc.psum_pool(name="banks", bufs=8))
        ctx.enter_context(tc.manual_schedule())

        warm = keep.tile([P, 1], F32, name="warm")
        nc.vector.memset(warm[:], 0.0)
        nc.scalar.activation(out=warm[:], in_=warm[:], func=COPY)
        identity = keep.tile([P, P], F32, name="identity")
        make_identity(nc, identity[:])
        identity16 = keep.tile([P, P], BF16, name="identity16")
        nc.gpsimd.tensor_copy(out=identity16[:], in_=identity[:])
        psi_rows = keep.tile([P, P], BF16, name="psi_rows")
        nc.gpsimd.memset(psi_rows[:], 0.0)

        scale_cols = keep.tile([P, D // P], F32, name="scale_cols")
        nc.sync.dma_start(out=scale_cols[:], in_=x_scale.rearrange("o (p m) -> p (o m)", p=P))
        r16 = keep.tile([P, GROUPS, PACK], BF16, name="r16")
        nc.scalar.dma_start(out=r16[:], in_=r.rearrange("(g p t) -> p g t", p=P, t=PACK))
        t16 = keep.tile([P, GROUPS, PACK], BF16, name="t16")
        nc.scalar.dma_start(out=t16[:], in_=t.rearrange("(g p t) -> p g t", p=P, t=PACK))

        x_view = x_bytes.rearrange("(g p t) f -> g p t f", p=P, t=PACK)
        p_view = p.rearrange("(g p j) d -> g p j d", p=P, j=PACK)
        beta_view = beta.rearrange("(g p j) d -> g p j d", p=P, j=PACK)
        x_raw = []
        for g in range(GROUPS):
            raw = keep.tile([P, PACK, D], U8, name=f"x_raw{g}")
            x_raw.append(raw)
        w_raw = {}
        for b in range(BLOCKS):
            for g in range(PASSES):
                if (b, g) != (0, 0):
                    raw = keep.tile([P, PACK, WIDTH], BF16, name=f"w_raw{b}{g}")
                    w_raw[b, g] = raw
        first_halves = []
        for half in range(2):
            raw = keep.tile([P, PACK, HALF], BF16, name=f"first_half{half}")
            first_halves.append(raw)

        def load_x(g, a, b):
            nc.sync.dma_start(out=x_raw[g][:, a:b, :], in_=x_view[g][:, a:b, :])

        def load_w(b, g):
            src = beta_view[g] if b == Z else p_view[g][:, :, b * WIDTH : (b + 1) * WIDTH]
            nc.sync.dma_start(out=w_raw[b, g][:], in_=src)

        def load_first(half):
            cols = slice(half * HALF, (half + 1) * HALF)
            nc.sync.dma_start(out=first_halves[half][:], in_=p_view[0][:, :, cols])

        load_first(0)
        load_x(0, 0, 2)
        load_first(1)
        load_w(0, 1)
        load_x(0, 2, 4)
        load_w(Z, 0)
        load_w(Z, 1)
        load_x(1, 0, 4)
        load_w(1, 0)
        load_w(1, 1)
        load_x(2, 0, 4)
        load_x(3, 0, 4)
        nc.sync.dma_start(out=psi_rows[0:D_BLOCKS, :], in_=psi.rearrange("(b p) -> b p", p=P))
        v_raw = keep.tile([P, D_BLOCKS, K], BF16, name="v_raw")
        nc.sync.dma_start(out=v_raw[:], in_=v.rearrange("(b p) k -> p b k", p=P))

        scale = keep.tile([P, D], F32, name="scale")
        w_codes = keep.tile([P, BLOCKS, PASSES, WIDTH], U32, name="w_codes", align_bytes=256)
        w_planes = keep.tile([P, BLOCKS, PASSES, WIDTH], U8, name="w_planes", align_bytes=256)
        x_codes = keep.tile([P, UNITS, PASSES, P], U32, name="x_codes", align_bytes=256)
        x_planes = keep.tile([P, UNITS, PASSES, P], U8, name="x_planes", align_bytes=256)
        y_codes = keep.tile([P, GROUPS, BLOCKS, WIDTH], U32, name="y_codes", align_bytes=256)
        y_planes = keep.tile([P, GROUPS, BLOCKS, WIDTH], U8, name="y_planes", align_bytes=256)
        factor_r = keep.tile([P, UNITS], F32, name="factor_r")
        factor_t = keep.tile([P, UNITS], F32, name="factor_t")
        psi_inv = keep.tile([P, D_BLOCKS], F32, name="psi_inv")
        psi_inv_mean = keep.tile([P, D_BLOCKS], F32, name="psi_inv_mean")
        v_scaled = keep.tile([P, D_BLOCKS - FIRST_SCALED_V, K], F32, name="v_scaled")

        w_grouped, wide, turned, x_grouped = {}, {}, {}, {}
        y_bank, y_flat, y_grouped = {}, {}, {}
        vector_copy = nc.vector.tensor_copy
        scalar_copy = nc.scalar.copy

        def spread_scale():
            view = scale[:].rearrange("p (n q m) -> p q n m", q=2, m=4)
            for q, copy in ((0, vector_copy), (1, scalar_copy)):
                bank = banks.tile([P, 4, P], F32, name="bank")
                for m in range(4):
                    col = scale_cols[:, 4 * q + m : 4 * q + m + 1]
                    nc.tensor.transpose(bank[:, m, :], col.to_broadcast([P, P]), identity[:])
                copy(out=view[:, q], in_=bank[:].rearrange("p m n -> p n m"))

        def interleave(copy, dst, src):
            copy(
                out=dst.rearrange("p (c i) j -> p c j i", i=4),
                in_=src.rearrange("p j (c i) -> p c j i", i=4),
            )

        def w_group_first(half):
            if half == 0:
                tile = work.tile([P, WIDTH, PACK], BF16, name="w_grouped_tile", bufs=5, align_bytes=256)
                w_grouped[0, 0] = tile
            dst = w_grouped[0, 0][:, half * HALF : (half + 1) * HALF, :]
            interleave(vector_copy, dst, first_halves[half][:])

        def w_group(b, g, copy):
            tile = work.tile([P, WIDTH, PACK], BF16, name="w_grouped_tile", bufs=5, align_bytes=256)
            interleave(copy, tile[:], w_raw[b, g][:])
            w_grouped[b, g] = tile

        def w_quantize(b, g):
            nc.vector.quantize_mx(
                out=w_codes[:, b, g, :].bitcast(FP8X4),
                scales=w_planes[:, b, g, :],
                in_=w_grouped[b, g][:].rearrange("p c j -> p (c j)"),
            )

        def product(i):
            tile = work.tile([P, D], BF16, name="wide_tile", bufs=WIDE_BUFS)
            nc.vector.tensor_tensor(
                out=tile[:],
                in0=x_raw[i // PACK][:, i % PACK, :].bitcast(FP8),
                in1=scale[:],
                op=MULT,
            )
            wide[i] = tile

        def turn(i):
            bank = banks.tile([P, PASSES, 2, P], F32, name="bank")
            words = wide[i][:].bitcast(F32)
            for g in range(PASSES):
                for u in range(2):
                    nc.tensor.transpose(
                        bank[:, g, u, :], words[:, 256 * g + u : 256 * (g + 1) : 2], identity[:]
                    )
            turned[i] = bank

        def x_group(i):
            if i % 2 == 0:
                tile = work.tile([P, 2, PASSES * P * PACK], BF16, name="x_grouped_tile", align_bytes=256)
                x_grouped[i // 2] = tile
            nc.scalar.copy(
                out=x_grouped[i // 2][:, i % 2, :].bitcast(F32).rearrange("p (g c u) -> p g c u", g=PASSES, u=2),
                in_=turned[i][:].rearrange("p g u c -> p g c u"),
            )

        def x_quantize(k):
            nc.vector.quantize_mx(
                out=x_codes[:, 2 * k : 2 * k + 2].rearrange("p u g c -> p (u g c)").bitcast(FP8X4),
                scales=x_planes[:, 2 * k : 2 * k + 2].rearrange("p u g c -> p (u g c)"),
                in_=x_grouped[k][:].rearrange("p u n -> p (u n)"),
            )

        def multiply(i, b):
            bank = banks.tile([P, WIDTH], F32, name="bank")
            for g in range(PASSES):
                nc.tensor.matmul_mx(
                    out=bank[:],
                    lhsT=x_codes[:, i, g, :].bitcast(FP8X4),
                    lhsT_scale=x_planes[:, i, g, :],
                    rhs=w_codes[:, b, g, :].bitcast(FP8X4),
                    rhs_scale=w_planes[:, b, g, :],
                    start=(g == 0),
                    stop=(g == PASSES - 1),
                )
            y_bank[i, b] = bank

        def empty(i, b):
            group, j = i // PACK, i % PACK
            if j == 0:
                tile = work.tile([P, PACK, WIDTH], BF16, name=f"y_flat_tile{b}", bufs=2)
                y_flat[group, b] = tile
            factor = factor_t if b == Z else factor_r
            nc.scalar.activation(
                out=y_flat[group, b][:, j, :], in_=y_bank[i, b][:], func=COPY, scale=factor[:, i : i + 1]
            )

        def y_group(group, b):
            tile = work.tile([P, WIDTH, PACK], BF16, name="y_grouped_tile", align_bytes=256)
            interleave(vector_copy, tile[:], y_flat[group, b][:])
            y_grouped[group, b] = tile

        def y_quantize(group, b):
            nc.vector.quantize_mx(
                out=y_codes[:, group, b, :].bitcast(FP8X4),
                scales=y_planes[:, group, b, :],
                in_=y_grouped[group, b][:].rearrange("p c j -> p (c j)"),
            )

        def accumulate(bank, group, d):
            cols = slice(d % 4 * P, (d % 4 + 1) * P)
            nc.tensor.matmul_mx(
                out=bank[:],
                lhsT=y_codes[:, group, d // 4, cols].bitcast(FP8X4),
                lhsT_scale=y_planes[:, group, d // 4, cols],
                rhs=y_codes[:, group, Z, :].bitcast(FP8X4),
                rhs_scale=y_planes[:, group, Z, :],
                start=(group == 0),
                stop=(group == GROUPS - 1),
            )

        def prepare_psi():
            bank = banks.tile([P, P], BF16, name="bank")
            nc.tensor.transpose(bank[:], psi_rows[:], identity16[:])
            nc.vector.reciprocal(out=psi_inv[:], in_=bank[:, 0:D_BLOCKS])
            nc.vector.tensor_scalar(
                out=psi_inv_mean[:], in0=psi_inv[:], scalar1=1.0 / N, scalar2=None, op0=MULT
            )

        def prepare_v(d):
            nc.scalar.activation(
                out=v_scaled[:, d - FIRST_SCALED_V, :], in_=v_raw[:, d, :], func=COPY, scale=psi_inv[:, d : d + 1]
            )

        def finish(bank, d):
            tile = work.tile([P, K], F32, name="result", tag="wide_tile", bufs=WIDE_BUFS)
            if d < FIRST_SCALED_V:
                nc.vector.scalar_tensor_tensor(
                    out=tile[:], in0=bank[:], scalar=1.0 / N, in1=v_raw[:, d, :], op0=MULT, op1=SUBTRACT
                )
                nc.scalar.activation(out=tile[:], in_=tile[:], func=COPY, scale=psi_inv[:, d : d + 1])
            else:
                nc.vector.scalar_tensor_tensor(
                    out=tile[:],
                    in0=bank[:],
                    scalar=psi_inv_mean[:, d : d + 1],
                    in1=v_scaled[:, d - FIRST_SCALED_V, :],
                    op0=MULT,
                    op1=SUBTRACT,
                )
            nc.sync.dma_start(out=out[d * P : (d + 1) * P, :], in_=tile[:])

        calls = []

        def at(tick, kind, f, *args):
            calls.append((tick, KINDS.index(kind), len(calls), f, args))

        place = {}
        for g in range(GROUPS):
            for b in ORDER:
                for j in range(PACK):
                    shift = SHIFT[b] if g < GROUPS - 1 else 0
                    place[g * PACK + j, b] = len(place) + shift
        for b, g in W_AT:
            if (b, g) == (0, 0):
                at(W_AT[b, g], "w_group", w_group_first, 1)
            else:
                copy = scalar_copy
                at(W_AT[b, g], "w_group" if b != Z else "wz_group", w_group, b, g, copy)
            at(WQ_AT[b, g], "w_quantize", w_quantize, b, g)
        for i in range(UNITS):
            at(P_AT + P_STEP * i, "product", product, i)
            if i % 2 == 0:
                at(T_AT + T_STEP * (i + 1) + Q_LAG, "x_quantize", x_quantize, i // 2)
            at(T_AT + T_STEP * (i - i % 2), "turn", turn, i)
            at(T_AT + T_STEP * (i - i % 2), "x_group", x_group, i)
        for (i, b), n in place.items():
            at(n, "multiply", multiply, i, b)
            at(n, "empty", empty, i, b)
        for g in range(GROUPS):
            for b in ORDER:
                n = place[g * PACK + PACK - 1, b] + I_LAG
                at(n, "y_group", y_group, g, b)
                at(n + Y_LAG, "y_quantize", y_quantize, g, b)
        at(PSI_AT, "psi", prepare_psi)

        w_group_first(0)
        spread_scale()
        vector_copy(out=factor_r[:], in_=r16[:].rearrange("p g t -> p (g t)"))
        vector_copy(out=factor_t[:], in_=t16[:].rearrange("p g t -> p (g t)"))
        for tick, kind, n, f, args in sorted(calls, key=lambda c: c[:3]):
            f(*args)

        for d in range(FIRST_SCALED_V, D_BLOCKS):
            prepare_v(d)
        first = []
        for d in range(4):
            bank = banks.tile([P, K], F32, name="bank")
            first.append(bank)
        for g in range(GROUPS):
            for d in range(4):
                accumulate(first[d], g, d)
        for d in range(4):
            finish(first[d], d)
        for d in range(4, D_BLOCKS):
            bank = banks.tile([P, K], F32, name="bank")
            for g in range(GROUPS):
                accumulate(bank, g, d)
            finish(bank, d)
